import numpy as np
import ml_dtypes


def mxq(x, axis, fmt="e4m3"):
    dtype, down = {"e4m3": (ml_dtypes.float8_e4m3fn, 7), "e5m2": (ml_dtypes.float8_e5m2, 14)}[fmt]
    v = np.moveaxis(np.asarray(x, np.float32).astype(ml_dtypes.bfloat16).astype(np.float64), axis, -1)
    blocks = v.reshape(v.shape[:-1] + (-1, 32))
    amax = np.abs(blocks).max(-1, keepdims=True)
    byte = np.maximum(np.where(amax > 0, np.frexp(amax)[1] - 1 + 127, 0) - down, 1)
    scale = np.exp2(byte - 127.0)
    codes = (blocks / scale).astype(np.float32).astype(dtype).astype(np.float64)
    return np.moveaxis((codes * scale).reshape(v.shape), -1, axis)


WIDE = False


def mx_kscale(k):
    if not WIDE:
        return np.ones(k)
    levels = np.array([10, -10, 5, -5, 0])
    if k % 512:
        return np.exp2(np.random.permutation(np.resize(levels, k // 32))).repeat(32)
    a = np.empty((k // 512, 16))
    for p in range(k // 512):
        a[p, :8] = np.random.permutation(np.resize(levels, 8))
        for g in range(8):
            far = levels[np.abs(levels - a[p, g]) >= 10]
            a[p, g + 8] = far[np.random.randint(len(far))]
    return np.exp2(a.ravel()).repeat(32)


def f64(x):
    return np.asarray(x).astype(np.float64)


def striped(idx):
    return np.tile(idx.reshape(-1, 16).T, (8, 1)).astype(np.uint16)


def unstriped(offs):
    return offs[:16].T.reshape(-1).astype(np.int64)


def striped8(idx):
    return np.concatenate([x.reshape(-1, 16).T for x in idx]).astype(np.uint16)


def runs(offs, k):
    lists = np.stack([offs[16 * r : 16 * r + 16].T.reshape(-1) for r in range(8)]).astype(np.int64)
    return lists[np.arange(k) % 512 // 64]


def pack_weight(w):
    k, n = w.shape
    w = f64(np.asarray(w, np.float32).astype(ml_dtypes.bfloat16)).reshape(k // 32, 32, n)
    amax = np.abs(w).max(1)
    byte = np.clip(np.where(amax > 0, np.frexp(amax)[1] - 1 + 127 - 7, 1), 1, 254)
    scaled = (w * np.exp2(127.0 - byte)[:, None, :]).reshape(k, n).astype(np.float32)
    words = np.ascontiguousarray(scaled.reshape(k // 512, 128, 4, n).transpose(0, 1, 3, 2)).astype(ml_dtypes.float8_e4m3fn).view(np.uint8)
    return words, np.ascontiguousarray(byte.astype(np.uint8).reshape(k // 512, 16, n))


def unpack_weight(words, scales):
    g, p, n, _ = words.shape
    vals = np.ascontiguousarray(words).view(ml_dtypes.float8_e4m3fn).astype(np.float64) * np.repeat(np.exp2(scales.astype(np.float64) - 127.0), 8, axis=1)[..., None]
    return vals.transpose(0, 1, 3, 2).reshape(g * 512, n)


E2M1 = np.array([0.0, 0.5, 1.0, 1.5, 2.0, 3.0, 4.0, 6.0, -0.0, -0.5, -1.0, -1.5, -2.0, -3.0, -4.0, -6.0])


def pack_fp4(w):
    k, n = w.shape
    w = f64(np.asarray(w, np.float32).astype(ml_dtypes.bfloat16)).reshape(k // 32, 32, n)
    amax = np.abs(w).max(1)
    mant, ex = np.frexp(amax / 6.0)
    byte = np.clip(np.where(amax > 0, np.where(mant > 0.5, ex, ex - 1) + 127, 1), 1, 254)
    scaled = (w * np.exp2(127.0 - byte)[:, None, :]).reshape(k, n).astype(np.float32)
    c = np.ascontiguousarray(scaled.reshape(k // 512, 128, 4, n).transpose(0, 1, 3, 2)).astype(ml_dtypes.float4_e2m1fn).view(np.uint8) & 0xF
    words = (c[..., 0::2] | (c[..., 1::2] << 4)).reshape(k // 512, 128, 2 * n)
    return np.ascontiguousarray(words), np.ascontiguousarray(byte.astype(np.uint8).reshape(k // 512, 16, n))


def unpack_fp4(words, scales):
    g, _, n = scales.shape
    words = np.ascontiguousarray(words).reshape(g, 128, n, 2)
    nib = np.empty((g, 128, n, 4), np.uint8)
    nib[..., 0::2] = words & 0xF
    nib[..., 1::2] = words >> 4
    vals = E2M1[nib] * np.repeat(np.exp2(scales.astype(np.float64) - 127.0), 8, axis=1)[..., None]
    return vals.transpose(0, 1, 3, 2).reshape(g * 512, n)


def relu(v):
    return np.maximum(v, 0.0)

def planes(y):
    n, m = y.shape
    v = y.astype(np.float32).astype(ml_dtypes.bfloat16).astype(np.float64).reshape(n // 32, 32, m)
    top = np.abs(v).max(1)
    byte = np.clip(np.where(top > 0, np.frexp(top)[1] - 1 + 127 - 7, 1), 1, 254)
    codes = (v * np.exp2(127.0 - byte)[:, None, :]).reshape(n, m).astype(np.float32).astype(ml_dtypes.float8_e4m3fn).view(np.uint8)
    words = codes.reshape(n // 512, 128, 4, m).transpose(0, 1, 3, 2)
    return np.ascontiguousarray(words), np.ascontiguousarray(byte.astype(np.uint8).reshape(n // 512, 16, m))


K, T, S, N, H = 512, 2048, 512, 512, 512


def setup_inputs():
    n = np.random.standard_normal
    s = mx_kscale(K)[:, None]
    u = mx_kscale(H)
    packed_xT = pack_weight(n((K, T)) * s)
    packed_w1 = pack_fp4(n((K, H)) / np.sqrt(K) / s)
    packed_w2 = pack_fp4(n((H, N)) / np.sqrt(H) / u[:, None])
    return {
        "x_words": packed_xT[0],
        "x_scales": packed_xT[1],
        "w1_words": packed_w1[0],
        "w1_scales": packed_w1[1],
        "gn": (np.random.uniform(0.5, 1.5, (H, 1)) * u[:, None]).astype(np.float32),
        "w2_words": packed_w2[0],
        "w2_scales": packed_w2[1],
        "offs": striped(np.random.permutation(T)[:S]),
        "n1": striped8(np.stack([np.random.permutation(S) for _ in range(8)])),
        "n2": striped8(np.stack([np.random.permutation(S) for _ in range(8)])),
        "n3": striped8(np.stack([np.random.permutation(S) for _ in range(8)])),
        "n4": striped8(np.stack([np.random.permutation(S) for _ in range(8)])),
    }


def reference(x_words, x_scales, w1_words, w1_scales, gn, w2_words, w2_scales, offs, n1, n2, n3, n4):
    xq = unpack_weight(x_words, x_scales)[:, unstriped(offs)]
    y = unpack_fp4(w1_words, w1_scales).T @ xq
    a = y[np.arange(H)[:, None], runs(n1, H)]
    b = y[np.arange(H)[:, None], runs(n2, H)]
    c = y[np.arange(H)[:, None], runs(n3, H)]
    z = f64(gn) * (np.maximum(np.maximum(a, b), c) - (0.5 * (np.minimum(np.minimum(a, b), c))))
    h = unpack_fp4(w2_words, w2_scales).T @ mxq(z, 0, "e4m3")
    out_0 = h + -0.5 * (relu(h[np.arange(N)[:, None], runs(n4, N)]))
    return (out_0,) + planes(out_0)

@@ -1,0 +1,211 @@
+from contextlib import ExitStack
+
+import concourse.mybir as mybir
+
+K, T, S, N, H = 512, 2048, 512, 512, 512
+FLOPS = 2 * K * H * S + 2 * H * N * S
+
+F32 = mybir.dt.float32
+BF16 = mybir.dt.bfloat16
+I32 = mybir.dt.int32
+U32 = mybir.dt.uint32
+U16 = mybir.dt.uint16
+U8 = mybir.dt.uint8
+FP8X4 = mybir.dt.float8_e4m3fn_x4
+FP4X4 = mybir.dt.float4_e2m1fn_x4
+ALU = mybir.AluOpType
+ACT = mybir.ActivationFunctionType
+
+P = 128
+PACK = 4
+BANK = 512
+CHUNKS = ((0, 256), (256, 128), (384, 128))
+
+
+def tile_picked_rangelay_none_po_kernel(
+    tc, x_words, x_scales, w1_words, w1_scales, gn, w2_words, w2_scales, offs, n1, n2, n3, n4, out_0, out_1, out_2
+):
+    nc = tc.nc
+    with ExitStack() as ctx:
+        lists = ctx.enter_context(tc.tile_pool(name="lists", bufs=1))
+        keep = ctx.enter_context(tc.tile_pool(name="keep", bufs=1))
+        psum = ctx.enter_context(tc.psum_pool(name="psum", bufs=8))
+
+        def kept(shape, dtype, name):
+            return keep.tile(shape, dtype, name=name, align_bytes=64)
+
+        def bank():
+            return psum.tile([P, BANK], F32, name="bank")
+
+        def load_scale_rows(queues, plane, rows):
+            for q in range(4):
+                queues[q].dma_start(out=plane[32 * q : 32 * q + 4, :].bitcast(I32), in_=rows[0, 4 * q : 4 * q + 4, :].bitcast(I32))
+
+        def load_list(name, src):
+            tile = lists.tile([P, S // 16], U16, name=name)
+            nc.sync.dma_start(tile[:], src)
+            return tile
+
+        def entries(tile, start, width):
+            return tile[:, start // 16 : (start + width) // 16]
+
+        x_plane = kept([P, T], U8, "x_plane")
+        w1_plane_raw = kept([P, H], U8, "w1_plane_raw")
+        w2_plane_raw = kept([P, N], U8, "w2_plane_raw")
+        x_rows = kept([P, T // 4], I32, "x_rows")
+        nc.vector.memset(w1_plane_raw[:].bitcast(I32), 0)
+        nc.vector.memset(x_plane[:].bitcast(I32), 0)
+        nc.vector.memset(w2_plane_raw[:].bitcast(I32), 0)
+
+        for q in range(4):
+            queue = nc.sync if q < 2 else nc.scalar
+            queue.dma_start(out=x_rows[32 * q : 32 * q + 4, :], in_=x_scales[0, 4 * q : 4 * q + 4, :].bitcast(I32))
+        x_codes = kept([P, T], I32, "x_codes")
+        nc.sync.dma_start(out=x_codes[:], in_=x_words[0].rearrange("p n t -> p (n t)").bitcast(I32))
+        offs_t = load_list("offs_t", offs)
+        w1_raw = kept([P, 2 * H], U8, "w1_raw")
+        nc.gpsimd.dma_start(out=w1_raw[:].bitcast(I32), in_=w1_words[0].bitcast(I32))
+        load_scale_rows((nc.scalar, nc.scalar, nc.gpsimd, nc.gpsimd), w1_plane_raw, w1_scales)
+        gain = kept([P, PACK], F32, "gain")
+        nc.gpsimd.dma_start(out=gain[:], in_=gn.rearrange("(p t) o -> p (t o)", t=PACK))
+        n1_t = load_list("n1_t", n1)
+        n2_t = load_list("n2_t", n2)
+        n3_t = load_list("n3_t", n3)
+        n4_t = load_list("n4_t", n4)
+        w2_raw = kept([P, 2 * N], U8, "w2_raw")
+        nc.gpsimd.dma_start(out=w2_raw[:].bitcast(I32), in_=w2_words[0].bitcast(I32))
+        load_scale_rows((nc.gpsimd,) * 4, w2_plane_raw, w2_scales)
+        for q in range(4):
+            nc.vector.tensor_copy(out=x_plane[32 * q : 32 * q + 4, :].bitcast(I32), in_=x_rows[32 * q : 32 * q + 4, :])
+
+        def deal(raw, plane_raw, name):
+            codes = kept([P, 2 * H], U8, name + "_codes")
+            plane = kept([P, H], U8, name + "_plane")
+            nc.vector.tensor_copy(
+                out=codes[:].rearrange("p (t m b) -> p m t b", t=PACK, b=2),
+                in_=raw[:].rearrange("p (m t b) -> p m t b", t=PACK, b=2),
+            )
+            nc.vector.tensor_copy(
+                out=plane[:].rearrange("p (t m) -> p m t", t=PACK),
+                in_=plane_raw[:].rearrange("p (m t) -> p m t", t=PACK),
+            )
+            return codes, plane
+
+        def product(acc, codes, plane, t, moving, moving_plane):
+            nc.tensor.matmul_mx(
+                out=acc,
+                lhsT=codes[:, 2 * P * t : 2 * P * (t + 1)].bitcast(FP4X4),
+                lhsT_scale=plane[:, P * t : P * (t + 1)],
+                rhs=moving.bitcast(FP8X4),
+                rhs_scale=moving_plane,
+                start=True,
+                stop=True,
+            )
+
+        xg_plane = kept([P, S], U8, "xg_plane")
+        nc.vector.tensor_copy(out=xg_plane[:], in_=x_plane[:].indirect(offs_t[:]))
+        w1_codes, w1_plane = deal(w1_raw, w1_plane_raw, "w1")
+
+        three_if_up = kept([P, PACK], F32, "three_if_up")
+        nc.vector.tensor_scalar(out=three_if_up[:], in0=gain[:], scalar1=0.0, scalar2=3.0, op0=ALU.is_ge, op1=ALU.mult)
+        c_max = kept([P, PACK], F32, "c_max")
+        c_min = kept([P, PACK], F32, "c_min")
+        nc.vector.tensor_scalar(out=c_max[:], in0=three_if_up[:], scalar1=1.0, scalar2=-1.0, op0=ALU.mult, op1=ALU.add)
+        nc.vector.tensor_scalar(out=c_min[:], in0=three_if_up[:], scalar1=-1.0, scalar2=2.0, op0=ALU.mult, op1=ALU.add)
+
+        xg_codes = kept([P, S], U32, "xg_codes")
+        half = S // 2
+        for u in range(2):
+            nc.vector.tensor_copy(
+                out=xg_codes[:, half * u : half * (u + 1)],
+                in_=x_codes[:].bitcast(U32).indirect(entries(offs_t, half * u, half)),
+            )
+
+        y_win = [kept([P, S], F32, "y_win%d" % t) for t in range(PACK)]
+        pieces = [(0, 0, half), (0, half, half)] + [(t, 0, S) for t in range(1, PACK)]
+        for t, start, width in pieces:
+            cols = slice(start, start + width)
+            acc = bank()
+            product(acc[:, :width], w1_codes, w1_plane, t, xg_codes[:, cols], xg_plane[:, cols])
+            nc.scalar.activation(out=y_win[t][:, cols], in_=acc[:, :width], func=ACT.Copy, scale=gain[:, t : t + 1])
+
+        w2_codes, w2_plane = deal(w2_raw, w2_plane_raw, "w2")
+
+        h_rows = kept([P, PACK, S], F32, "h_rows")
+        h_win = [kept([P, S], F32, "h_win%d" % t) for t in range(PACK)]
+        z_codes = kept([P, S], U32, "z_codes")
+        z_plane = kept([P, S], U8, "z_plane")
+
+        def round_and_weave(on_vector, rows, factor, width, name):
+            woven = kept([P, width * PACK], BF16, name)
+            dst = woven[:].rearrange("p (c i t) -> p c t i", i=4, t=PACK)
+            src = rows.rearrange("p t (c i) -> p c t i", i=4)
+            if on_vector:
+                nc.vector.tensor_scalar(out=dst, in0=src, scalar1=factor, scalar2=None, op0=ALU.mult)
+            else:
+                nc.scalar.activation(out=dst, in_=src, func=ACT.Copy, scale=factor)
+            return woven
+
+        for n, (start, width) in enumerate(CHUNKS):
+            cols = slice(start, start + width)
+            last = n == len(CHUNKS) - 1
+            a, d1, d2, hi, lo, part, z = [kept([P, PACK, width], F32, "%s%d" % (s, n)) for s in ("a", "d1_", "d2_", "hi", "lo", "part", "z")]
+            for pair in range(2):
+                ts = (2 * pair, 2 * pair + 1)
+                both = slice(ts[0], ts[1] + 1)
+                for t in ts:
+                    nc.vector.tensor_copy(out=a[:, t, :], in_=y_win[t][:].indirect(entries(n1_t, start, width)))
+                for d, lst in ((d1, n2_t), (d2, n3_t)):
+                    for t in ts:
+                        nc.vector.tensor_tensor(
+                            out=d[:, t, :], in0=y_win[t][:].indirect(entries(lst, start, width)), in1=a[:, t, :], op=ALU.subtract
+                        )
+                for ext, op in ((hi, ALU.max), (lo, ALU.min)):
+                    nc.vector.scalar_tensor_tensor(
+                        out=ext[:, both, :], in0=d1[:, both, :], scalar=0.0, in1=d2[:, both, :], op0=op, op1=op
+                    )
+                for dst, ext, coef, base in ((part, hi, c_max, a), (z, lo, c_min, part)):
+                    for t in ts:
+                        nc.vector.scalar_tensor_tensor(
+                            out=dst[:, t, :], in0=ext[:, t, :], scalar=coef[:, t : t + 1], in1=base[:, t, :], op0=ALU.mult, op1=ALU.add
+                        )
+            z_woven = round_and_weave(last, z[:], 0.5, width, "z_woven%d" % n)
+            nc.vector.quantize_mx(out=z_codes[:, cols].bitcast(FP8X4), scales=z_plane[:, cols], in_=z_woven[:])
+
+            per_bank = BANK // width
+            for t0 in range(0, PACK, per_bank):
+                acc = bank()
+                for i in range(per_bank):
+                    product(acc[:, width * i : width * (i + 1)], w2_codes, w2_plane, t0 + i, z_codes[:, cols], z_plane[:, cols])
+                if last:
+                    for i in range(per_bank):
+                        nc.vector.tensor_scalar(
+                            out=h_win[t0 + i][:, cols], in0=acc[:, width * i : width * (i + 1)],
+                            scalar1=0.0, scalar2=-0.5, op0=ALU.max, op1=ALU.mult,
+                        )
+                nc.scalar.copy(out=h_rows[:, t0 : t0 + per_bank, cols], in_=acc[:].rearrange("p (i j) -> p i j", i=per_bank))
+                if not last:
+                    pos = kept([P, BANK], F32, "pos%d_%d" % (n, t0))
+                    nc.scalar.activation(out=pos[:], in_=acc[:], func=ACT.Relu, scale=0.5)
+                    for i in range(per_bank):
+                        nc.scalar.activation(out=h_win[t0 + i][:, cols], in_=pos[:, width * i : width * (i + 1)], func=ACT.Copy, scale=-1.0)
+
+        out_rows = out_0.rearrange("(p t) s -> p t s", t=PACK)
+        out_words = out_1[0].rearrange("p n t -> p (n t)").bitcast(I32)
+        o_codes = kept([P, S], I32, "o_codes")
+        o_plane = kept([P, S], U8, "o_plane")
+        for n, (start, width) in enumerate(CHUNKS):
+            cols = slice(start, start + width)
+            last = n == len(CHUNKS) - 1
+            o = kept([P, PACK, width], F32, "o%d" % n)
+            for t in range(PACK):
+                nc.vector.tensor_tensor(
+                    out=o[:, t, :], in0=h_win[t][:].indirect(entries(n4_t, start, width)), in1=h_rows[:, t, cols], op=ALU.add
+                )
+            (nc.scalar if last else nc.sync).dma_start(out=out_rows[:, :, cols], in_=o[:])
+            o_woven = round_and_weave(last, o[:], 1.0, width, "o_woven%d" % n)
+            nc.vector.quantize_mx(out=o_codes[:, cols].bitcast(FP8X4), scales=o_plane[:, cols], in_=o_woven[:])
+            nc.sync.dma_start(out=out_words[:, cols], in_=o_codes[:, cols])
+        for q in range(4):
+            queue = nc.sync if q % 2 == 0 else nc.scalar
+            queue.dma_start(out=out_2[0, 4 * q : 4 * q + 4, :].bitcast(I32), in_=o_plane[32 * q : 32 * q + 4, :].bitcast(I32))

@@ -31,15 +31,15 @@ def tile_picked_rangelay_none_po_kernel(
         keep = ctx.enter_context(tc.tile_pool(name="keep", bufs=1))
         psum = ctx.enter_context(tc.psum_pool(name="psum", bufs=8))
 
-        def kept(shape, dtype, name):
-            return keep.tile(shape, dtype, name=name, align_bytes=64)
+        def kept(shape, dtype, name, tag=None):
+            return keep.tile(shape, dtype, name=name, tag=tag or name, align_bytes=64)
 
         def bank():
             return psum.tile([P, BANK], F32, name="bank")
 
-        def load_scale_rows(queues, plane, rows):
+        def load_scale_rows(queues, words, rows):
             for q in range(4):
-                queues[q].dma_start(out=plane[32 * q : 32 * q + 4, :].bitcast(I32), in_=rows[0, 4 * q : 4 * q + 4, :].bitcast(I32))
+                queues[q].dma_start(out=words[32 * q : 32 * q + 4, :], in_=rows[0, 4 * q : 4 * q + 4, :].bitcast(I32))
 
         def load_list(name, src):
             tile = lists.tile([P, S // 16], U16, name=name)
@@ -53,34 +53,34 @@ def tile_picked_rangelay_none_po_kernel(
         w1_plane_raw = kept([P, H], U8, "w1_plane_raw")
         w2_plane_raw = kept([P, N], U8, "w2_plane_raw")
         x_rows = kept([P, T // 4], I32, "x_rows")
-        nc.vector.memset(w1_plane_raw[:].bitcast(I32), 0)
+        nc.gpsimd.memset(w1_plane_raw[:].bitcast(I32), 0)
         nc.vector.memset(x_plane[:].bitcast(I32), 0)
         nc.vector.memset(w2_plane_raw[:].bitcast(I32), 0)
 
-        for q in range(4):
-            queue = nc.sync if q < 2 else nc.scalar
-            queue.dma_start(out=x_rows[32 * q : 32 * q + 4, :], in_=x_scales[0, 4 * q : 4 * q + 4, :].bitcast(I32))
-        x_codes = kept([P, T], I32, "x_codes")
-        nc.sync.dma_start(out=x_codes[:], in_=x_words[0].rearrange("p n t -> p (n t)").bitcast(I32))
+        load_scale_rows((nc.sync, nc.sync, nc.scalar, nc.scalar), x_rows[:], x_scales)
         offs_t = load_list("offs_t", offs)
         w1_raw = kept([P, 2 * H], U8, "w1_raw")
-        nc.gpsimd.dma_start(out=w1_raw[:].bitcast(I32), in_=w1_words[0].bitcast(I32))
-        load_scale_rows((nc.scalar, nc.scalar, nc.gpsimd, nc.gpsimd), w1_plane_raw, w1_scales)
+        nc.scalar.dma_start(out=w1_raw[:].bitcast(I32), in_=w1_words[0].bitcast(I32))
+        x_codes = kept([P, T], I32, "x_codes")
+        nc.sync.dma_start(out=x_codes[:], in_=x_words[0].rearrange("p n t -> p (n t)").bitcast(I32))
         gain = kept([P, PACK], F32, "gain")
-        nc.gpsimd.dma_start(out=gain[:], in_=gn.rearrange("(p t) o -> p (t o)", t=PACK))
+        nc.scalar.dma_start(out=gain[:], in_=gn.rearrange("(p t) o -> p (t o)", t=PACK))
+        load_scale_rows((nc.gpsimd,) * 4, w1_plane_raw[:].bitcast(I32), w1_scales)
         n1_t = load_list("n1_t", n1)
         n2_t = load_list("n2_t", n2)
         n3_t = load_list("n3_t", n3)
         n4_t = load_list("n4_t", n4)
         w2_raw = kept([P, 2 * N], U8, "w2_raw")
-        nc.gpsimd.dma_start(out=w2_raw[:].bitcast(I32), in_=w2_words[0].bitcast(I32))
-        load_scale_rows((nc.gpsimd,) * 4, w2_plane_raw, w2_scales)
-        for q in range(4):
-            nc.vector.tensor_copy(out=x_plane[32 * q : 32 * q + 4, :].bitcast(I32), in_=x_rows[32 * q : 32 * q + 4, :])
+        nc.sync.dma_start(out=w2_raw[:].bitcast(I32), in_=w2_words[0].bitcast(I32))
+        load_scale_rows((nc.sync,) * 4, w2_plane_raw[:].bitcast(I32), w2_scales)
 
-        def deal(raw, plane_raw, name):
-            codes = kept([P, 2 * H], U8, name + "_codes")
-            plane = kept([P, H], U8, name + "_plane")
+        def place_scale_rows(rows, plane):
+            for q in range(4):
+                nc.vector.tensor_copy(out=plane[32 * q : 32 * q + 4, :].bitcast(I32), in_=rows[32 * q : 32 * q + 4, :])
+
+        def deal(raw, plane_raw, name, codes_tag):
+            codes = kept([P, 2 * H], U8, name + "_codes", codes_tag)
+            plane = kept([P, H], U8, name + "_plane", "w_plane")
             nc.vector.tensor_copy(
                 out=codes[:].rearrange("p (t m b) -> p m t b", t=PACK, b=2),
                 in_=raw[:].rearrange("p (m t b) -> p m t b", t=PACK, b=2),
@@ -102,9 +102,10 @@ def tile_picked_rangelay_none_po_kernel(
                 stop=True,
             )
 
+        place_scale_rows(x_rows, x_plane)
         xg_plane = kept([P, S], U8, "xg_plane")
         nc.vector.tensor_copy(out=xg_plane[:], in_=x_plane[:].indirect(offs_t[:]))
-        w1_codes, w1_plane = deal(w1_raw, w1_plane_raw, "w1")
+        w1_codes, w1_plane = deal(w1_raw, w1_plane_raw, "w1", "w1_codes")
 
         three_if_up = kept([P, PACK], F32, "three_if_up")
         nc.vector.tensor_scalar(out=three_if_up[:], in0=gain[:], scalar1=0.0, scalar2=3.0, op0=ALU.is_ge, op1=ALU.mult)
@@ -129,7 +130,7 @@ def tile_picked_rangelay_none_po_kernel(
             product(acc[:, :width], w1_codes, w1_plane, t, xg_codes[:, cols], xg_plane[:, cols])
             nc.scalar.activation(out=y_win[t][:, cols], in_=acc[:, :width], func=ACT.Copy, scale=gain[:, t : t + 1])
 
-        w2_codes, w2_plane = deal(w2_raw, w2_plane_raw, "w2")
+        w2_codes, w2_plane = deal(w2_raw, w2_plane_raw, "w2", "x_codes")
 
         h_rows = kept([P, PACK, S], F32, "h_rows")
         h_win = [kept([P, S], F32, "h_win%d" % t) for t in range(PACK)]

@@ -1,6 +1,7 @@
 from contextlib import ExitStack
 
 import concourse.mybir as mybir
+from concourse.masks import make_identity
 
 K, T, S, N, H = 512, 2048, 512, 512, 512
 FLOPS = 2 * K * H * S + 2 * H * N * S
@@ -19,7 +20,8 @@ ACT = mybir.ActivationFunctionType
 P = 128
 PACK = 4
 BANK = 512
-CHUNKS = ((0, 256), (256, 128), (384, 128))
+HALF = S // 2
+OUT_CHUNKS = ((0, 256), (256, 128), (384, 128))
 
 
 def tile_picked_rangelay_none_po_kernel(
@@ -29,7 +31,8 @@ def tile_picked_rangelay_none_po_kernel(
     with ExitStack() as ctx:
         lists = ctx.enter_context(tc.tile_pool(name="lists", bufs=1))
         keep = ctx.enter_context(tc.tile_pool(name="keep", bufs=1))
-        psum = ctx.enter_context(tc.psum_pool(name="psum", bufs=8))
+        psum = ctx.enter_context(tc.psum_pool(name="psum", bufs=4))
+        psum_t = ctx.enter_context(tc.psum_pool(name="psum_t", bufs=2))
 
         def kept(shape, dtype, name, tag=None):
             return keep.tile(shape, dtype, name=name, tag=tag or name, align_bytes=64)
@@ -37,9 +40,9 @@ def tile_picked_rangelay_none_po_kernel(
         def bank():
             return psum.tile([P, BANK], F32, name="bank")
 
-        def load_scale_rows(queues, words, rows):
+        def load_scale_rows(queues, plane, rows):
             for q in range(4):
-                queues[q].dma_start(out=words[32 * q : 32 * q + 4, :], in_=rows[0, 4 * q : 4 * q + 4, :].bitcast(I32))
+                queues[q].dma_start(out=plane[32 * q : 32 * q + 4, :].bitcast(I32), in_=rows[0, 4 * q : 4 * q + 4, :].bitcast(I32))
 
         def load_list(name, src):
             tile = lists.tile([P, S // 16], U16, name=name)
@@ -52,44 +55,43 @@ def tile_picked_rangelay_none_po_kernel(
         x_plane = kept([P, T], U8, "x_plane")
         w1_plane_raw = kept([P, H], U8, "w1_plane_raw")
         w2_plane_raw = kept([P, N], U8, "w2_plane_raw")
-        x_rows = kept([P, T // 4], I32, "x_rows")
-        nc.gpsimd.memset(w1_plane_raw[:].bitcast(I32), 0)
-        nc.vector.memset(x_plane[:].bitcast(I32), 0)
-        nc.vector.memset(w2_plane_raw[:].bitcast(I32), 0)
+        for plane in (x_plane, w1_plane_raw, w2_plane_raw):
+            nc.vector.memset(plane[:].bitcast(I32), 0)
+        ident = kept([P, P], F32, "ident")
+        make_identity(nc, ident[:])
 
-        load_scale_rows((nc.sync, nc.sync, nc.scalar, nc.scalar), x_rows[:], x_scales)
         offs_t = load_list("offs_t", offs)
         w1_raw = kept([P, 2 * H], U8, "w1_raw")
         nc.scalar.dma_start(out=w1_raw[:].bitcast(I32), in_=w1_words[0].bitcast(I32))
-        x_codes = kept([P, T], I32, "x_codes")
-        nc.sync.dma_start(out=x_codes[:], in_=x_words[0].rearrange("p n t -> p (n t)").bitcast(I32))
+        w2_raw = kept([P, 2 * N], U8, "w2_raw")
+        nc.gpsimd.dma_start(out=w2_raw[:].bitcast(I32), in_=w2_words[0].bitcast(I32))
+        n1_t = load_list("n1_t", n1)
         gain = kept([P, PACK], F32, "gain")
         nc.scalar.dma_start(out=gain[:], in_=gn.rearrange("(p t) o -> p (t o)", t=PACK))
-        load_scale_rows((nc.gpsimd,) * 4, w1_plane_raw[:].bitcast(I32), w1_scales)
-        n1_t = load_list("n1_t", n1)
         n2_t = load_list("n2_t", n2)
         n3_t = load_list("n3_t", n3)
+        x_codes = kept([P, T], I32, "x_codes")
+        nc.sync.dma_start(out=x_codes[:], in_=x_words[0].rearrange("p n t -> p (n t)").bitcast(I32))
         n4_t = load_list("n4_t", n4)
-        w2_raw = kept([P, 2 * N], U8, "w2_raw")
-        nc.sync.dma_start(out=w2_raw[:].bitcast(I32), in_=w2_words[0].bitcast(I32))
-        load_scale_rows((nc.sync,) * 4, w2_plane_raw[:].bitcast(I32), w2_scales)
+        load_scale_rows((nc.sync,) * 4, x_plane, x_scales)
+        load_scale_rows((nc.sync, nc.sync, nc.gpsimd, nc.gpsimd), w1_plane_raw, w1_scales)
+        load_scale_rows((nc.sync,) * 4, w2_plane_raw, w2_scales)
 
-        def place_scale_rows(rows, plane):
-            for q in range(4):
-                nc.vector.tensor_copy(out=plane[32 * q : 32 * q + 4, :].bitcast(I32), in_=rows[32 * q : 32 * q + 4, :])
-
-        def deal(raw, plane_raw, name, codes_tag):
-            codes = kept([P, 2 * H], U8, name + "_codes", codes_tag)
-            plane = kept([P, H], U8, name + "_plane", "w_plane")
+        def deal_codes(raw, name):
+            codes = kept([P, 2 * H], U8, name)
             nc.vector.tensor_copy(
                 out=codes[:].rearrange("p (t m b) -> p m t b", t=PACK, b=2),
                 in_=raw[:].rearrange("p (m t b) -> p m t b", t=PACK, b=2),
             )
+            return codes
+
+        def deal_plane(raw, name, tag):
+            plane = kept([P, H], U8, name, tag)
             nc.vector.tensor_copy(
                 out=plane[:].rearrange("p (t m) -> p m t", t=PACK),
-                in_=plane_raw[:].rearrange("p (m t) -> p m t", t=PACK),
+                in_=raw[:].rearrange("p (m t) -> p m t", t=PACK),
             )
-            return codes, plane
+            return plane
 
         def product(acc, codes, plane, t, moving, moving_plane):
             nc.tensor.matmul_mx(
@@ -102,10 +104,8 @@ def tile_picked_rangelay_none_po_kernel(
                 stop=True,
             )
 
-        place_scale_rows(x_rows, x_plane)
-        xg_plane = kept([P, S], U8, "xg_plane")
-        nc.vector.tensor_copy(out=xg_plane[:], in_=x_plane[:].indirect(offs_t[:]))
-        w1_codes, w1_plane = deal(w1_raw, w1_plane_raw, "w1", "w1_codes")
+        w1_codes = deal_codes(w1_raw, "w1_codes")
+        w2_codes = deal_codes(w2_raw, "w2_codes")
 
         three_if_up = kept([P, PACK], F32, "three_if_up")
         nc.vector.tensor_scalar(out=three_if_up[:], in0=gain[:], scalar1=0.0, scalar2=3.0, op0=ALU.is_ge, op1=ALU.mult)
@@ -114,97 +114,157 @@ def tile_picked_rangelay_none_po_kernel(
         nc.vector.tensor_scalar(out=c_max[:], in0=three_if_up[:], scalar1=1.0, scalar2=-1.0, op0=ALU.mult, op1=ALU.add)
         nc.vector.tensor_scalar(out=c_min[:], in0=three_if_up[:], scalar1=-1.0, scalar2=2.0, op0=ALU.mult, op1=ALU.add)
 
+        halves = [slice(HALF * g, HALF * (g + 1)) for g in range(2)]
         xg_codes = kept([P, S], U32, "xg_codes")
-        half = S // 2
-        for u in range(2):
-            nc.vector.tensor_copy(
-                out=xg_codes[:, half * u : half * (u + 1)],
-                in_=x_codes[:].bitcast(U32).indirect(entries(offs_t, half * u, half)),
-            )
+        xg_plane = kept([P, S], U8, "xg_plane")
+        w1_plane = deal_plane(w1_plane_raw, "w1_plane", None)
+        for g in range(2):
+            nc.vector.tensor_copy(out=xg_codes[:, halves[g]], in_=x_codes[:].bitcast(U32).indirect(entries(offs_t, HALF * g, HALF)))
+            nc.vector.tensor_copy(out=xg_plane[:, halves[g]], in_=x_plane[:].indirect(entries(offs_t, HALF * g, HALF)))
+        w2_plane = deal_plane(w2_plane_raw, "w2_plane", "x_plane")
 
         y_win = [kept([P, S], F32, "y_win%d" % t) for t in range(PACK)]
-        pieces = [(0, 0, half), (0, half, half)] + [(t, 0, S) for t in range(1, PACK)]
-        for t, start, width in pieces:
-            cols = slice(start, start + width)
+        for t, cols in [(t, cols) for cols in halves for t in range(2)] + [(t, slice(0, S)) for t in range(2, PACK)]:
+            width = cols.stop - cols.start
             acc = bank()
             product(acc[:, :width], w1_codes, w1_plane, t, xg_codes[:, cols], xg_plane[:, cols])
             nc.scalar.activation(out=y_win[t][:, cols], in_=acc[:, :width], func=ACT.Copy, scale=gain[:, t : t + 1])
-
-        w2_codes, w2_plane = deal(w2_raw, w2_plane_raw, "w2", "x_codes")
 
         h_rows = kept([P, PACK, S], F32, "h_rows")
         h_win = [kept([P, S], F32, "h_win%d" % t) for t in range(PACK)]
         z_codes = kept([P, S], U32, "z_codes")
         z_plane = kept([P, S], U8, "z_plane")
+        z_woven = [kept([P, HALF, PACK], BF16, "z_woven%d" % g) for g in range(2)]
 
-        def round_and_weave(on_vector, rows, factor, width, name):
-            woven = kept([P, width * PACK], BF16, name)
-            dst = woven[:].rearrange("p (c i t) -> p c t i", i=4, t=PACK)
-            src = rows.rearrange("p t (c i) -> p c t i", i=4)
-            if on_vector:
-                nc.vector.tensor_scalar(out=dst, in0=src, scalar1=factor, scalar2=None, op0=ALU.mult)
-            else:
-                nc.scalar.activation(out=dst, in_=src, func=ACT.Copy, scale=factor)
-            return woven
-
-        for n, (start, width) in enumerate(CHUNKS):
-            cols = slice(start, start + width)
-            last = n == len(CHUNKS) - 1
-            a, d1, d2, hi, lo, part, z = [kept([P, PACK, width], F32, "%s%d" % (s, n)) for s in ("a", "d1_", "d2_", "hi", "lo", "part", "z")]
-            for pair in range(2):
-                ts = (2 * pair, 2 * pair + 1)
-                both = slice(ts[0], ts[1] + 1)
-                for t in ts:
-                    nc.vector.tensor_copy(out=a[:, t, :], in_=y_win[t][:].indirect(entries(n1_t, start, width)))
-                for d, lst in ((d1, n2_t), (d2, n3_t)):
-                    for t in ts:
-                        nc.vector.tensor_tensor(
-                            out=d[:, t, :], in0=y_win[t][:].indirect(entries(lst, start, width)), in1=a[:, t, :], op=ALU.subtract
-                        )
-                for ext, op in ((hi, ALU.max), (lo, ALU.min)):
-                    nc.vector.scalar_tensor_tensor(
-                        out=ext[:, both, :], in0=d1[:, both, :], scalar=0.0, in1=d2[:, both, :], op0=op, op1=op
+        def spread(g, u, a_tag=None, d1_tag=None, d2_tag=None):
+            name = "%d_%d" % (g, u)
+            a = kept([P, 2, HALF], F32, "a" + name, a_tag)
+            d1 = kept([P, 2, HALF], F32, "d1_" + name, d1_tag)
+            d2 = kept([P, 2, HALF], F32, "d2_" + name, d2_tag)
+            hi, lo = [kept([P, 2, HALF], F32, s + name) for s in ("hi", "lo")]
+            for e in range(2):
+                nc.vector.tensor_copy(out=a[:, e, :], in_=y_win[2 * u + e][:].indirect(entries(n1_t, HALF * g, HALF)))
+            for d, lst in ((d1, n2_t), (d2, n3_t)):
+                for e in range(2):
+                    nc.vector.tensor_tensor(
+                        out=d[:, e, :], in0=y_win[2 * u + e][:].indirect(entries(lst, HALF * g, HALF)), in1=a[:, e, :], op=ALU.subtract
                     )
-                for dst, ext, coef, base in ((part, hi, c_max, a), (z, lo, c_min, part)):
-                    for t in ts:
-                        nc.vector.scalar_tensor_tensor(
-                            out=dst[:, t, :], in0=ext[:, t, :], scalar=coef[:, t : t + 1], in1=base[:, t, :], op0=ALU.mult, op1=ALU.add
-                        )
-            z_woven = round_and_weave(last, z[:], 0.5, width, "z_woven%d" % n)
-            nc.vector.quantize_mx(out=z_codes[:, cols].bitcast(FP8X4), scales=z_plane[:, cols], in_=z_woven[:])
+            for ext, op in ((hi, ALU.max), (lo, ALU.min)):
+                nc.vector.scalar_tensor_tensor(out=ext[:], in0=d1[:], scalar=0.0, in1=d2[:], op0=op, op1=op)
+            return a, hi, lo
 
-            per_bank = BANK // width
-            for t0 in range(0, PACK, per_bank):
-                acc = bank()
-                for i in range(per_bank):
-                    product(acc[:, width * i : width * (i + 1)], w2_codes, w2_plane, t0 + i, z_codes[:, cols], z_plane[:, cols])
-                if last:
-                    for i in range(per_bank):
-                        nc.vector.tensor_scalar(
-                            out=h_win[t0 + i][:, cols], in0=acc[:, width * i : width * (i + 1)],
-                            scalar1=0.0, scalar2=-0.5, op0=ALU.max, op1=ALU.mult,
+        def sum_on_tensor(g, u, a, hi, lo, scaled_tag=None):
+            name = "%d_%d" % (g, u)
+            scaled = kept([P, 2, 2, HALF], F32, "scaled" + name, scaled_tag)
+            hi_c, lo_c = scaled[:, 0, :, :], scaled[:, 1, :, :]
+            total = psum_t.tile([P, 2, 2, P], F32, name="total")
+            for e in range(2):
+                t = 2 * u + e
+                for ext_c, ext, coef in ((hi_c, hi, c_max), (lo_c, lo, c_min)):
+                    nc.scalar.activation(out=ext_c[:, e, :], in_=ext[:, e, :], func=ACT.Copy, scale=coef[:, t : t + 1])
+                for blk in range(2):
+                    for i, term in enumerate((a, hi_c, lo_c)):
+                        nc.tensor.matmul(
+                            total[:, blk, e, :], lhsT=term[:, e, P * blk : P * (blk + 1)], rhs=ident[:],
+                            is_transpose=True, start=(i == 0), stop=(i == 2),
                         )
-                nc.scalar.copy(out=h_rows[:, t0 : t0 + per_bank, cols], in_=acc[:].rearrange("p (i j) -> p i j", i=per_bank))
-                if not last:
-                    pos = kept([P, BANK], F32, "pos%d_%d" % (n, t0))
-                    nc.scalar.activation(out=pos[:], in_=acc[:], func=ACT.Relu, scale=0.5)
-                    for i in range(per_bank):
-                        nc.scalar.activation(out=h_win[t0 + i][:, cols], in_=pos[:, width * i : width * (i + 1)], func=ACT.Copy, scale=-1.0)
+            return total
+
+        def turn_back(g, u, total, back):
+            z_t = kept([P, 2, P, 2], BF16, "z_t%d_%d" % (g, u))
+            nc.scalar.activation(out=z_t[:], in_=total[:].rearrange("j b e p -> j b p e"), func=ACT.Copy, scale=0.5)
+            z_t_words = z_t[:].rearrange("j b p e -> j (b p e)").bitcast(F32)
+            for blk in range(2):
+                nc.tensor.transpose(back[:, u, P * blk : P * (blk + 1)], z_t_words[:, P * blk : P * (blk + 1)], ident[:])
+
+        def woven_words(g):
+            return z_woven[g][:].rearrange("p j t -> p (j t)").bitcast(F32).rearrange("p (j u) -> p j u", u=2)
+
+        def sum_on_vector(g, u, a, hi, lo):
+            part, z = [kept([P, 2, HALF], F32, s) for s in ("part", "z")]
+            for e in range(2):
+                t = 2 * u + e
+                nc.vector.scalar_tensor_tensor(
+                    out=part[:, e, :], in0=hi[:, e, :], scalar=c_max[:, t : t + 1], in1=a[:, e, :], op0=ALU.mult, op1=ALU.add
+                )
+            for blk in range(2):
+                js = slice(P * blk, P * (blk + 1))
+                for e in range(2):
+                    t = 2 * u + e
+                    nc.vector.scalar_tensor_tensor(
+                        out=z[:, e, js], in0=lo[:, e, js], scalar=c_min[:, t : t + 1], in1=part[:, e, js], op0=ALU.mult, op1=ALU.add
+                    )
+            for blk in range(2):
+                js = slice(P * blk, P * (blk + 1))
+                nc.vector.tensor_scalar(
+                    out=z_woven[g][:, js, 2 * u : 2 * u + 2], in0=z[:, :, js].rearrange("p e j -> p j e"),
+                    scalar1=0.5, scalar2=None, op0=ALU.mult,
+                )
+
+        def second_product(g, width):
+            accs = [bank() for u in range(2)]
+            for start in range(0, HALF, width):
+                cols = slice(HALF * g + start, HALF * g + start + width)
+                nc.vector.quantize_mx(
+                    out=z_codes[:, cols].bitcast(FP8X4), scales=z_plane[:, cols],
+                    in_=z_woven[g][:, start : start + width, :].rearrange("p j t -> p (j t)"),
+                )
+                for t in range(PACK):
+                    at = HALF * (t % 2) + start
+                    product(accs[t // 2][:, at : at + width], w2_codes, w2_plane, t, z_codes[:, cols], z_plane[:, cols])
+            return accs
+
+        def windows_on_scalar(g, u, acc):
+            pos = kept([P, BANK], F32, "pos%d_%d" % (g, u))
+            nc.scalar.activation(out=pos[:], in_=acc[:], func=ACT.Relu, scale=0.5)
+            for e in range(2):
+                nc.scalar.activation(out=h_win[2 * u + e][:, halves[g]], in_=pos[:, halves[e]], func=ACT.Copy, scale=-1.0)
+
+        def windows_on_vector(g, u, acc):
+            for e in range(2):
+                nc.vector.tensor_scalar(
+                    out=h_win[2 * u + e][:, halves[g]], in0=acc[:, halves[e]], scalar1=0.0, scalar2=-0.5, op0=ALU.max, op1=ALU.mult
+                )
+
+        def keep_h(g, accs):
+            for u in range(2):
+                nc.scalar.copy(out=h_rows[:, 2 * u : 2 * u + 2, halves[g]], in_=accs[u][:].rearrange("p (e j) -> p e j", e=2))
+
+        back0 = psum_t.tile([P, 2, HALF], F32, name="back")
+        for u in range(2):
+            turn_back(0, u, sum_on_tensor(0, u, *spread(0, u)), back0)
+        nc.scalar.copy(out=woven_words(0), in_=back0[:].rearrange("p u j -> p j u"))
+        third = spread(1, 0, a_tag="d1_0_0", d1_tag="d1_0_1", d2_tag="d2_0_1")
+        accs = second_product(0, HALF)
+        total = sum_on_tensor(1, 0, *third, scaled_tag="z_t0_1")
+        windows_on_scalar(0, 0, accs[0])
+        back1 = psum_t.tile([P, 2, HALF], F32, name="back")
+        turn_back(1, 0, total, back1)
+        windows_on_scalar(0, 1, accs[1])
+        nc.scalar.copy(out=woven_words(1)[:, :, 0], in_=back1[:, 0, :])
+        keep_h(0, accs)
+        sum_on_vector(1, 1, *spread(1, 1, d2_tag="z_woven0"))
+        accs = second_product(1, P)
+        windows_on_vector(1, 0, accs[0])
+        windows_on_scalar(1, 1, accs[1])
+        keep_h(1, accs)
 
         out_rows = out_0.rearrange("(p t) s -> p t s", t=PACK)
         out_words = out_1[0].rearrange("p n t -> p (n t)").bitcast(I32)
         o_codes = kept([P, S], I32, "o_codes")
         o_plane = kept([P, S], U8, "o_plane")
-        for n, (start, width) in enumerate(CHUNKS):
+        for n, (start, width) in enumerate(OUT_CHUNKS):
             cols = slice(start, start + width)
-            last = n == len(CHUNKS) - 1
             o = kept([P, PACK, width], F32, "o%d" % n)
             for t in range(PACK):
                 nc.vector.tensor_tensor(
                     out=o[:, t, :], in0=h_win[t][:].indirect(entries(n4_t, start, width)), in1=h_rows[:, t, cols], op=ALU.add
                 )
-            (nc.scalar if last else nc.sync).dma_start(out=out_rows[:, :, cols], in_=o[:])
-            o_woven = round_and_weave(last, o[:], 1.0, width, "o_woven%d" % n)
+            nc.sync.dma_start(out=out_rows[:, :, cols], in_=o[:])
+            o_woven = kept([P, width * PACK], BF16, "o_woven%d" % n)
+            nc.scalar.copy(
+                out=o_woven[:].rearrange("p (c i t) -> p c t i", i=4, t=PACK), in_=o[:].rearrange("p t (c i) -> p c t i", i=4)
+            )
             nc.vector.quantize_mx(out=o_codes[:, cols].bitcast(FP8X4), scales=o_plane[:, cols], in_=o_woven[:])
             nc.sync.dma_start(out=out_words[:, cols], in_=o_codes[:, cols])
         for q in range(4):

@@ -31,6 +31,7 @@ def tile_picked_rangelay_none_po_kernel(
     with ExitStack() as ctx:
         lists = ctx.enter_context(tc.tile_pool(name="lists", bufs=1))
         keep = ctx.enter_context(tc.tile_pool(name="keep", bufs=1))
+        shared = ctx.enter_context(tc.tile_pool(name="shared", bufs=1))
         psum = ctx.enter_context(tc.psum_pool(name="psum", bufs=4))
         psum_t = ctx.enter_context(tc.psum_pool(name="psum_t", bufs=2))
 
@@ -40,9 +41,9 @@ def tile_picked_rangelay_none_po_kernel(
         def bank():
             return psum.tile([P, BANK], F32, name="bank")
 
-        def load_scale_rows(queues, plane, rows):
+        def load_scale_rows(queues, words, rows):
             for q in range(4):
-                queues[q].dma_start(out=plane[32 * q : 32 * q + 4, :].bitcast(I32), in_=rows[0, 4 * q : 4 * q + 4, :].bitcast(I32))
+                queues[q].dma_start(out=words[32 * q : 32 * q + 4, :], in_=rows[0, 4 * q : 4 * q + 4, :].bitcast(I32))
 
         def load_list(name, src):
             tile = lists.tile([P, S // 16], U16, name=name)
@@ -55,43 +56,34 @@ def tile_picked_rangelay_none_po_kernel(
         x_plane = kept([P, T], U8, "x_plane")
         w1_plane_raw = kept([P, H], U8, "w1_plane_raw")
         w2_plane_raw = kept([P, N], U8, "w2_plane_raw")
-        for plane in (x_plane, w1_plane_raw, w2_plane_raw):
+        for plane in (w1_plane_raw, x_plane, w2_plane_raw):
             nc.vector.memset(plane[:].bitcast(I32), 0)
-        ident = kept([P, P], F32, "ident")
-        make_identity(nc, ident[:])
 
+        x_rows = kept([P, T // 4], I32, "x_rows")
+        load_scale_rows((nc.sync, nc.sync, nc.scalar, nc.scalar), x_rows[:], x_scales)
         offs_t = load_list("offs_t", offs)
+        gain = kept([P, PACK], F32, "gain")
+        nc.scalar.dma_start(out=gain[:], in_=gn.rearrange("(p t) o -> p (t o)", t=PACK))
         w1_raw = kept([P, 2 * H], U8, "w1_raw")
         nc.scalar.dma_start(out=w1_raw[:].bitcast(I32), in_=w1_words[0].bitcast(I32))
+        x_codes = shared.tile([P, T], I32, name="x_codes", align_bytes=64, offset=0)
+        nc.sync.dma_start(out=x_codes[:], in_=x_words[0].rearrange("p n t -> p (n t)").bitcast(I32))
         w2_raw = kept([P, 2 * N], U8, "w2_raw")
         nc.gpsimd.dma_start(out=w2_raw[:].bitcast(I32), in_=w2_words[0].bitcast(I32))
         n1_t = load_list("n1_t", n1)
-        gain = kept([P, PACK], F32, "gain")
-        nc.scalar.dma_start(out=gain[:], in_=gn.rearrange("(p t) o -> p (t o)", t=PACK))
         n2_t = load_list("n2_t", n2)
         n3_t = load_list("n3_t", n3)
-        x_codes = kept([P, T], I32, "x_codes")
-        nc.sync.dma_start(out=x_codes[:], in_=x_words[0].rearrange("p n t -> p (n t)").bitcast(I32))
         n4_t = load_list("n4_t", n4)
-        load_scale_rows((nc.sync,) * 4, x_plane, x_scales)
-        load_scale_rows((nc.sync, nc.sync, nc.gpsimd, nc.gpsimd), w1_plane_raw, w1_scales)
-        load_scale_rows((nc.sync,) * 4, w2_plane_raw, w2_scales)
+        load_scale_rows((nc.sync, nc.sync, nc.gpsimd, nc.gpsimd), w1_plane_raw[:].bitcast(I32), w1_scales)
+        load_scale_rows((nc.sync,) * 4, w2_plane_raw[:].bitcast(I32), w2_scales)
+        ident = kept([P, P], F32, "ident")
+        make_identity(nc, ident[:])
 
-        def deal_codes(raw, name):
-            codes = kept([P, 2 * H], U8, name)
+        def deal(dealt, raw, width):
             nc.vector.tensor_copy(
-                out=codes[:].rearrange("p (t m b) -> p m t b", t=PACK, b=2),
-                in_=raw[:].rearrange("p (m t b) -> p m t b", t=PACK, b=2),
+                out=dealt[:].rearrange("p (t m b) -> p t m b", t=PACK, b=width),
+                in_=raw[:].rearrange("p (m t b) -> p t m b", t=PACK, b=width),
             )
-            return codes
-
-        def deal_plane(raw, name, tag):
-            plane = kept([P, H], U8, name, tag)
-            nc.vector.tensor_copy(
-                out=plane[:].rearrange("p (t m) -> p m t", t=PACK),
-                in_=raw[:].rearrange("p (m t) -> p m t", t=PACK),
-            )
-            return plane
 
         def product(acc, codes, plane, t, moving, moving_plane):
             nc.tensor.matmul_mx(
@@ -104,8 +96,20 @@ def tile_picked_rangelay_none_po_kernel(
                 stop=True,
             )
 
-        w1_codes = deal_codes(w1_raw, "w1_codes")
-        w2_codes = deal_codes(w2_raw, "w2_codes")
+        w1_codes = kept([P, 2 * H], U8, "w1_codes")
+        deal(w1_codes, w1_raw, 2)
+        for q in range(4):
+            nc.vector.tensor_copy(out=x_plane[32 * q : 32 * q + 4, :].bitcast(I32), in_=x_rows[32 * q : 32 * q + 4, :])
+        xg_codes = kept([P, S], U32, "xg_codes")
+        xg_plane = kept([P, S], U8, "xg_plane")
+        nc.vector.tensor_copy(out=xg_plane[:], in_=x_plane[:].indirect(offs_t[:]))
+        nc.vector.tensor_copy(out=xg_codes[:], in_=x_codes[:].bitcast(U32).indirect(offs_t[:]))
+        w1_plane = shared.tile([P, H], U8, name="w1_plane", align_bytes=64, offset=0)
+        w2_codes = shared.tile([P, 2 * N], U8, name="w2_codes", align_bytes=64, offset=H)
+        w2_plane = shared.tile([P, N], U8, name="w2_plane", align_bytes=64, offset=H + 2 * N)
+        deal(w1_plane, w1_plane_raw, 1)
+        deal(w2_codes, w2_raw, 2)
+        deal(w2_plane, w2_plane_raw, 1)
 
         three_if_up = kept([P, PACK], F32, "three_if_up")
         nc.vector.tensor_scalar(out=three_if_up[:], in0=gain[:], scalar1=0.0, scalar2=3.0, op0=ALU.is_ge, op1=ALU.mult)
@@ -115,16 +119,9 @@ def tile_picked_rangelay_none_po_kernel(
         nc.vector.tensor_scalar(out=c_min[:], in0=three_if_up[:], scalar1=-1.0, scalar2=2.0, op0=ALU.mult, op1=ALU.add)
 
         halves = [slice(HALF * g, HALF * (g + 1)) for g in range(2)]
-        xg_codes = kept([P, S], U32, "xg_codes")
-        xg_plane = kept([P, S], U8, "xg_plane")
-        w1_plane = deal_plane(w1_plane_raw, "w1_plane", None)
-        for g in range(2):
-            nc.vector.tensor_copy(out=xg_codes[:, halves[g]], in_=x_codes[:].bitcast(U32).indirect(entries(offs_t, HALF * g, HALF)))
-            nc.vector.tensor_copy(out=xg_plane[:, halves[g]], in_=x_plane[:].indirect(entries(offs_t, HALF * g, HALF)))
-        w2_plane = deal_plane(w2_plane_raw, "w2_plane", "x_plane")
 
         y_win = [kept([P, S], F32, "y_win%d" % t) for t in range(PACK)]
-        for t, cols in [(t, cols) for cols in halves for t in range(2)] + [(t, slice(0, S)) for t in range(2, PACK)]:
+        for t, cols in [(t, cols) for t in range(2) for cols in halves] + [(t, slice(0, S)) for t in range(2, PACK)]:
             width = cols.stop - cols.start
             acc = bank()
             product(acc[:, :width], w1_codes, w1_plane, t, xg_codes[:, cols], xg_plane[:, cols])
@@ -153,9 +150,9 @@ def tile_picked_rangelay_none_po_kernel(
                 nc.vector.scalar_tensor_tensor(out=ext[:], in0=d1[:], scalar=0.0, in1=d2[:], op0=op, op1=op)
             return a, hi, lo
 
-        def sum_on_tensor(g, u, a, hi, lo, scaled_tag=None):
+        def sum_on_tensor(g, u, a, hi, lo):
             name = "%d_%d" % (g, u)
-            scaled = kept([P, 2, 2, HALF], F32, "scaled" + name, scaled_tag)
+            scaled = kept([P, 2, 2, HALF], F32, "scaled" + name)
             hi_c, lo_c = scaled[:, 0, :, :], scaled[:, 1, :, :]
             total = psum_t.tile([P, 2, 2, P], F32, name="total")
             for e in range(2):
@@ -180,26 +177,19 @@ def tile_picked_rangelay_none_po_kernel(
         def woven_words(g):
             return z_woven[g][:].rearrange("p j t -> p (j t)").bitcast(F32).rearrange("p (j u) -> p j u", u=2)
 
-        def sum_on_vector(g, u, a, hi, lo):
-            part, z = [kept([P, 2, HALF], F32, s) for s in ("part", "z")]
+        def sum_on_vector(u, z, blocks, a, hi, lo):
+            part = kept([P, 2, HALF], F32, "part%d" % u)
             for e in range(2):
                 t = 2 * u + e
                 nc.vector.scalar_tensor_tensor(
                     out=part[:, e, :], in0=hi[:, e, :], scalar=c_max[:, t : t + 1], in1=a[:, e, :], op0=ALU.mult, op1=ALU.add
                 )
-            for blk in range(2):
-                js = slice(P * blk, P * (blk + 1))
+            for js in blocks:
                 for e in range(2):
                     t = 2 * u + e
                     nc.vector.scalar_tensor_tensor(
-                        out=z[:, e, js], in0=lo[:, e, js], scalar=c_min[:, t : t + 1], in1=part[:, e, js], op0=ALU.mult, op1=ALU.add
+                        out=z[:, t, js], in0=lo[:, e, js], scalar=c_min[:, t : t + 1], in1=part[:, e, js], op0=ALU.mult, op1=ALU.add
                     )
-            for blk in range(2):
-                js = slice(P * blk, P * (blk + 1))
-                nc.vector.tensor_scalar(
-                    out=z_woven[g][:, js, 2 * u : 2 * u + 2], in0=z[:, :, js].rearrange("p e j -> p j e"),
-                    scalar1=0.5, scalar2=None, op0=ALU.mult,
-                )
 
         def second_product(g, width):
             accs = [bank() for u in range(2)]
@@ -230,20 +220,24 @@ def tile_picked_rangelay_none_po_kernel(
             for u in range(2):
                 nc.scalar.copy(out=h_rows[:, 2 * u : 2 * u + 2, halves[g]], in_=accs[u][:].rearrange("p (e j) -> p e j", e=2))
 
-        back0 = psum_t.tile([P, 2, HALF], F32, name="back")
+        back = psum_t.tile([P, 2, HALF], F32, name="back")
         for u in range(2):
-            turn_back(0, u, sum_on_tensor(0, u, *spread(0, u)), back0)
-        nc.scalar.copy(out=woven_words(0), in_=back0[:].rearrange("p u j -> p j u"))
-        third = spread(1, 0, a_tag="d1_0_0", d1_tag="d1_0_1", d2_tag="d2_0_1")
+            turn_back(0, u, sum_on_tensor(0, u, *spread(0, u)), back)
+        nc.scalar.copy(out=woven_words(0), in_=back[:].rearrange("p u j -> p j u"))
+        z = kept([P, PACK, HALF], F32, "z")
+        blocks = [slice(P * blk, P * (blk + 1)) for blk in range(2)]
+        sum_on_vector(0, z, [slice(0, HALF)], *spread(1, 0, a_tag="d1_0_0", d1_tag="d1_0_1", d2_tag="d2_0_1"))
         accs = second_product(0, HALF)
-        total = sum_on_tensor(1, 0, *third, scaled_tag="z_t0_1")
-        windows_on_scalar(0, 0, accs[0])
-        back1 = psum_t.tile([P, 2, HALF], F32, name="back")
-        turn_back(1, 0, total, back1)
-        windows_on_scalar(0, 1, accs[1])
-        nc.scalar.copy(out=woven_words(1)[:, :, 0], in_=back1[:, 0, :])
+        for u in range(2):
+            windows_on_scalar(0, u, accs[u])
         keep_h(0, accs)
-        sum_on_vector(1, 1, *spread(1, 1, d2_tag="z_woven0"))
+        sum_on_vector(1, z, blocks, *spread(1, 1, d1_tag="z_woven0"))
+        for js in blocks:
+            nc.vector.tensor_scalar(
+                out=z_woven[1][:, js, :].rearrange("p (c i) t -> p c t i", i=4),
+                in0=z[:, :, js].rearrange("p t (c i) -> p c t i", i=4),
+                scalar1=0.5, scalar2=None, op0=ALU.mult,
+            )
         accs = second_product(1, P)
         windows_on_vector(1, 0, accs[0])
         windows_on_scalar(1, 1, accs[1])

@@ -19,8 +19,10 @@ ACT = mybir.ActivationFunctionType
 
 P = 128
 PACK = 4
+QUADRANTS = 4
 BANK = 512
 HALF = S // 2
+RUN = 4
 OUT_CHUNKS = ((0, 256), (256, 128), (384, 128))
 
 
@@ -42,7 +44,7 @@ def tile_picked_rangelay_none_po_kernel(
             return psum.tile([P, BANK], F32, name="bank")
 
         def load_scale_rows(queues, words, rows):
-            for q in range(4):
+            for q in range(QUADRANTS):
                 queues[q].dma_start(out=words[32 * q : 32 * q + 4, :], in_=rows[0, 4 * q : 4 * q + 4, :].bitcast(I32))
 
         def load_list(name, src):
@@ -75,7 +77,7 @@ def tile_picked_rangelay_none_po_kernel(
         n3_t = load_list("n3_t", n3)
         n4_t = load_list("n4_t", n4)
         load_scale_rows((nc.sync, nc.sync, nc.gpsimd, nc.gpsimd), w1_plane_raw[:].bitcast(I32), w1_scales)
-        load_scale_rows((nc.sync,) * 4, w2_plane_raw[:].bitcast(I32), w2_scales)
+        load_scale_rows((nc.sync,) * QUADRANTS, w2_plane_raw[:].bitcast(I32), w2_scales)
         ident = kept([P, P], F32, "ident")
         make_identity(nc, ident[:])
 
@@ -98,7 +100,7 @@ def tile_picked_rangelay_none_po_kernel(
 
         w1_codes = kept([P, 2 * H], U8, "w1_codes")
         deal(w1_codes, w1_raw, 2)
-        for q in range(4):
+        for q in range(QUADRANTS):
             nc.vector.tensor_copy(out=x_plane[32 * q : 32 * q + 4, :].bitcast(I32), in_=x_rows[32 * q : 32 * q + 4, :])
         xg_codes = kept([P, S], U32, "xg_codes")
         xg_plane = kept([P, S], U8, "xg_plane")
@@ -174,74 +176,76 @@ def tile_picked_rangelay_none_po_kernel(
             for blk in range(2):
                 nc.tensor.transpose(back[:, u, P * blk : P * (blk + 1)], z_t_words[:, P * blk : P * (blk + 1)], ident[:])
 
-        def woven_words(g):
-            return z_woven[g][:].rearrange("p j t -> p (j t)").bitcast(F32).rearrange("p (j u) -> p j u", u=2)
-
-        def sum_on_vector(u, z, blocks, a, hi, lo):
+        def sum_on_vector(u, twice_z, pieces, a, hi, lo):
             part = kept([P, 2, HALF], F32, "part%d" % u)
             for e in range(2):
                 t = 2 * u + e
                 nc.vector.scalar_tensor_tensor(
                     out=part[:, e, :], in0=hi[:, e, :], scalar=c_max[:, t : t + 1], in1=a[:, e, :], op0=ALU.mult, op1=ALU.add
                 )
-            for js in blocks:
+            for js in pieces:
                 for e in range(2):
                     t = 2 * u + e
                     nc.vector.scalar_tensor_tensor(
-                        out=z[:, t, js], in0=lo[:, e, js], scalar=c_min[:, t : t + 1], in1=part[:, e, js], op0=ALU.mult, op1=ALU.add
+                        out=twice_z[:, t, js], in0=lo[:, e, js], scalar=c_min[:, t : t + 1], in1=part[:, e, js], op0=ALU.mult, op1=ALU.add
                     )
 
-        def second_product(g, width):
-            accs = [bank() for u in range(2)]
-            for start in range(0, HALF, width):
-                cols = slice(HALF * g + start, HALF * g + start + width)
-                nc.vector.quantize_mx(
-                    out=z_codes[:, cols].bitcast(FP8X4), scales=z_plane[:, cols],
-                    in_=z_woven[g][:, start : start + width, :].rearrange("p j t -> p (j t)"),
-                )
-                for t in range(PACK):
-                    at = HALF * (t % 2) + start
-                    product(accs[t // 2][:, at : at + width], w2_codes, w2_plane, t, z_codes[:, cols], z_plane[:, cols])
-            return accs
+        def second_product(g, start, width):
+            cols = slice(HALF * g + start, HALF * g + start + width)
+            nc.vector.quantize_mx(
+                out=z_codes[:, cols].bitcast(FP8X4), scales=z_plane[:, cols],
+                in_=z_woven[g][:, start : start + width, :].rearrange("p j t -> p (j t)"),
+            )
+            accs = []
+            for u in range(2):
+                acc = bank()[:][:, : 2 * width].rearrange("p (e j) -> p e j", e=2)
+                for e in range(2):
+                    product(acc[:, e, :], w2_codes, w2_plane, 2 * u + e, z_codes[:, cols], z_plane[:, cols])
+                accs.append(acc)
+            return cols, accs
 
-        def windows_on_scalar(g, u, acc):
-            pos = kept([P, BANK], F32, "pos%d_%d" % (g, u))
-            nc.scalar.activation(out=pos[:], in_=acc[:], func=ACT.Relu, scale=0.5)
+        def windows_on_scalar(u, cols, acc):
+            pos = kept([P, 2, cols.stop - cols.start], F32, "pos%d_%d" % (cols.start, u))
+            nc.scalar.activation(out=pos[:], in_=acc, func=ACT.Relu, scale=0.5)
             for e in range(2):
-                nc.scalar.activation(out=h_win[2 * u + e][:, halves[g]], in_=pos[:, halves[e]], func=ACT.Copy, scale=-1.0)
+                nc.scalar.activation(out=h_win[2 * u + e][:, cols], in_=pos[:, e, :], func=ACT.Copy, scale=-1.0)
 
-        def windows_on_vector(g, u, acc):
+        def windows_on_vector(u, cols, acc):
             for e in range(2):
                 nc.vector.tensor_scalar(
-                    out=h_win[2 * u + e][:, halves[g]], in0=acc[:, halves[e]], scalar1=0.0, scalar2=-0.5, op0=ALU.max, op1=ALU.mult
+                    out=h_win[2 * u + e][:, cols], in0=acc[:, e, :], scalar1=0.0, scalar2=-0.5, op0=ALU.max, op1=ALU.mult
                 )
 
-        def keep_h(g, accs):
+        def keep_h(cols, accs):
             for u in range(2):
-                nc.scalar.copy(out=h_rows[:, 2 * u : 2 * u + 2, halves[g]], in_=accs[u][:].rearrange("p (e j) -> p e j", e=2))
+                nc.scalar.copy(out=h_rows[:, 2 * u : 2 * u + 2, cols], in_=accs[u])
 
         back = psum_t.tile([P, 2, HALF], F32, name="back")
         for u in range(2):
             turn_back(0, u, sum_on_tensor(0, u, *spread(0, u)), back)
-        nc.scalar.copy(out=woven_words(0), in_=back[:].rearrange("p u j -> p j u"))
-        z = kept([P, PACK, HALF], F32, "z")
+        woven_words = z_woven[0][:].rearrange("p j t -> p (j t)").bitcast(F32).rearrange("p (j u) -> p j u", u=2)
+        nc.scalar.copy(out=woven_words, in_=back[:].rearrange("p u j -> p j u"))
+
+        twice_z = kept([P, PACK, HALF], F32, "z")
         blocks = [slice(P * blk, P * (blk + 1)) for blk in range(2)]
-        sum_on_vector(0, z, [slice(0, HALF)], *spread(1, 0, a_tag="d1_0_0", d1_tag="d1_0_1", d2_tag="d2_0_1"))
-        accs = second_product(0, HALF)
+        sum_on_vector(0, twice_z, [slice(0, HALF)], *spread(1, 0, a_tag="d1_0_0", d1_tag="d1_0_1", d2_tag="d2_0_1"))
+        cols, accs = second_product(0, 0, HALF)
         for u in range(2):
-            windows_on_scalar(0, u, accs[u])
-        keep_h(0, accs)
-        sum_on_vector(1, z, blocks, *spread(1, 1, d1_tag="z_woven0"))
+            windows_on_scalar(u, cols, accs[u])
+        keep_h(cols, accs)
+        sum_on_vector(1, twice_z, blocks, *spread(1, 1, d1_tag="z_woven0"))
         for js in blocks:
             nc.vector.tensor_scalar(
-                out=z_woven[1][:, js, :].rearrange("p (c i) t -> p c t i", i=4),
-                in0=z[:, :, js].rearrange("p t (c i) -> p c t i", i=4),
+                out=z_woven[1][:, js, :].rearrange("p (c i) t -> p c t i", i=RUN),
+                in0=twice_z[:, :, js].rearrange("p t (c i) -> p c t i", i=RUN),
                 scalar1=0.5, scalar2=None, op0=ALU.mult,
             )
-        accs = second_product(1, P)
-        windows_on_vector(1, 0, accs[0])
-        windows_on_scalar(1, 1, accs[1])
-        keep_h(1, accs)
+        late = [second_product(1, js.start, P) for js in blocks]
+        for cols, accs in late:
+            windows_on_vector(0, cols, accs[0])
+            windows_on_scalar(1, cols, accs[1])
+        for cols, accs in late:
+            keep_h(cols, accs)
 
         out_rows = out_0.rearrange("(p t) s -> p t s", t=PACK)
         out_words = out_1[0].rearrange("p n t -> p (n t)").bitcast(I32)
@@ -257,10 +261,10 @@ def tile_picked_rangelay_none_po_kernel(
             nc.sync.dma_start(out=out_rows[:, :, cols], in_=o[:])
             o_woven = kept([P, width * PACK], BF16, "o_woven%d" % n)
             nc.scalar.copy(
-                out=o_woven[:].rearrange("p (c i t) -> p c t i", i=4, t=PACK), in_=o[:].rearrange("p t (c i) -> p c t i", i=4)
+                out=o_woven[:].rearrange("p (c i t) -> p c t i", i=RUN, t=PACK), in_=o[:].rearrange("p t (c i) -> p c t i", i=RUN)
             )
             nc.vector.quantize_mx(out=o_codes[:, cols].bitcast(FP8X4), scales=o_plane[:, cols], in_=o_woven[:])
             nc.sync.dma_start(out=out_words[:, cols], in_=o_codes[:, cols])
-        for q in range(4):
+        for q in range(QUADRANTS):
             queue = nc.sync if q % 2 == 0 else nc.scalar
             queue.dma_start(out=out_2[0, 4 * q : 4 * q + 4, :].bitcast(I32), in_=o_plane[32 * q : 32 * q + 4, :].bitcast(I32))

from contextlib import ExitStack

import concourse.mybir as mybir
from concourse.masks import make_identity

K, T, S, N, H = 512, 2048, 512, 512, 512
FLOPS = 2 * K * H * S + 2 * H * N * S

F32 = mybir.dt.float32
BF16 = mybir.dt.bfloat16
I32 = mybir.dt.int32
U32 = mybir.dt.uint32
U16 = mybir.dt.uint16
U8 = mybir.dt.uint8
FP8X4 = mybir.dt.float8_e4m3fn_x4
FP4X4 = mybir.dt.float4_e2m1fn_x4
ALU = mybir.AluOpType
ACT = mybir.ActivationFunctionType

P = 128
PACK = 4
QUADRANTS = 4
BANK = 512
HALF = S // 2
RUN = 4
OUT_CHUNKS = ((0, 256), (256, 128), (384, 128))


def tile_picked_rangelay_none_po_kernel(
    tc, x_words, x_scales, w1_words, w1_scales, gn, w2_words, w2_scales, offs, n1, n2, n3, n4, out_0, out_1, out_2
):
    nc = tc.nc
    with ExitStack() as ctx:
        lists = ctx.enter_context(tc.tile_pool(name="lists", bufs=1))
        keep = ctx.enter_context(tc.tile_pool(name="keep", bufs=1))
        shared = ctx.enter_context(tc.tile_pool(name="shared", bufs=1))
        psum = ctx.enter_context(tc.psum_pool(name="psum", bufs=4))
        psum_t = ctx.enter_context(tc.psum_pool(name="psum_t", bufs=2))

        def kept(shape, dtype, name, tag=None):
            return keep.tile(shape, dtype, name=name, tag=tag or name, align_bytes=64)

        def bank():
            return psum.tile([P, BANK], F32, name="bank")

        def load_scale_rows(queues, words, rows):
            for q in range(QUADRANTS):
                queues[q].dma_start(out=words[32 * q : 32 * q + 4, :], in_=rows[0, 4 * q : 4 * q + 4, :].bitcast(I32))

        def load_list(name, src):
            tile = lists.tile([P, S // 16], U16, name=name)
            nc.sync.dma_start(tile[:], src)
            return tile

        def entries(tile, start, width):
            return tile[:, start // 16 : (start + width) // 16]

        x_plane = kept([P, T], U8, "x_plane")
        w1_plane_raw = kept([P, H], U8, "w1_plane_raw")
        w2_plane_raw = kept([P, N], U8, "w2_plane_raw")
        for plane in (w1_plane_raw, x_plane, w2_plane_raw):
            nc.vector.memset(plane[:].bitcast(I32), 0)

        x_rows = kept([P, T // 4], I32, "x_rows")
        load_scale_rows((nc.sync, nc.sync, nc.scalar, nc.scalar), x_rows[:], x_scales)
        offs_t = load_list("offs_t", offs)
        gain = kept([P, PACK], F32, "gain")
        nc.scalar.dma_start(out=gain[:], in_=gn.rearrange("(p t) o -> p (t o)", t=PACK))
        w1_raw = kept([P, 2 * H], U8, "w1_raw")
        nc.scalar.dma_start(out=w1_raw[:].bitcast(I32), in_=w1_words[0].bitcast(I32))
        x_codes = shared.tile([P, T], I32, name="x_codes", align_bytes=64, offset=0)
        nc.sync.dma_start(out=x_codes[:], in_=x_words[0].rearrange("p n t -> p (n t)").bitcast(I32))
        w2_raw = kept([P, 2 * N], U8, "w2_raw")
        nc.gpsimd.dma_start(out=w2_raw[:].bitcast(I32), in_=w2_words[0].bitcast(I32))
        n1_t = load_list("n1_t", n1)
        n2_t = load_list("n2_t", n2)
        n3_t = load_list("n3_t", n3)
        n4_t = load_list("n4_t", n4)
        load_scale_rows((nc.sync, nc.sync, nc.gpsimd, nc.gpsimd), w1_plane_raw[:].bitcast(I32), w1_scales)
        load_scale_rows((nc.sync,) * QUADRANTS, w2_plane_raw[:].bitcast(I32), w2_scales)
        ident = kept([P, P], F32, "ident")
        make_identity(nc, ident[:])

        def deal(dealt, raw, width):
            nc.vector.tensor_copy(
                out=dealt[:].rearrange("p (t m b) -> p t m b", t=PACK, b=width),
                in_=raw[:].rearrange("p (m t b) -> p t m b", t=PACK, b=width),
            )

        def product(acc, codes, plane, t, moving, moving_plane):
            nc.tensor.matmul_mx(
                out=acc,
                lhsT=codes[:, 2 * P * t : 2 * P * (t + 1)].bitcast(FP4X4),
                lhsT_scale=plane[:, P * t : P * (t + 1)],
                rhs=moving.bitcast(FP8X4),
                rhs_scale=moving_plane,
                start=True,
                stop=True,
            )

        w1_codes = kept([P, 2 * H], U8, "w1_codes")
        deal(w1_codes, w1_raw, 2)
        for q in range(QUADRANTS):
            nc.vector.tensor_copy(out=x_plane[32 * q : 32 * q + 4, :].bitcast(I32), in_=x_rows[32 * q : 32 * q + 4, :])
        xg_codes = kept([P, S], U32, "xg_codes")
        xg_plane = kept([P, S], U8, "xg_plane")
        nc.vector.tensor_copy(out=xg_plane[:], in_=x_plane[:].indirect(offs_t[:]))
        nc.vector.tensor_copy(out=xg_codes[:], in_=x_codes[:].bitcast(U32).indirect(offs_t[:]))
        w1_plane = shared.tile([P, H], U8, name="w1_plane", align_bytes=64, offset=0)
        w2_codes = shared.tile([P, 2 * N], U8, name="w2_codes", align_bytes=64, offset=H)
        w2_plane = shared.tile([P, N], U8, name="w2_plane", align_bytes=64, offset=H + 2 * N)
        deal(w1_plane, w1_plane_raw, 1)
        deal(w2_codes, w2_raw, 2)
        deal(w2_plane, w2_plane_raw, 1)

        three_if_up = kept([P, PACK], F32, "three_if_up")
        nc.vector.tensor_scalar(out=three_if_up[:], in0=gain[:], scalar1=0.0, scalar2=3.0, op0=ALU.is_ge, op1=ALU.mult)
        c_max = kept([P, PACK], F32, "c_max")
        c_min = kept([P, PACK], F32, "c_min")
        nc.vector.tensor_scalar(out=c_max[:], in0=three_if_up[:], scalar1=1.0, scalar2=-1.0, op0=ALU.mult, op1=ALU.add)
        nc.vector.tensor_scalar(out=c_min[:], in0=three_if_up[:], scalar1=-1.0, scalar2=2.0, op0=ALU.mult, op1=ALU.add)

        halves = [slice(HALF * g, HALF * (g + 1)) for g in range(2)]

        y_win = [kept([P, S], F32, "y_win%d" % t) for t in range(PACK)]
        for t, cols in [(t, cols) for t in range(2) for cols in halves] + [(t, slice(0, S)) for t in range(2, PACK)]:
            width = cols.stop - cols.start
            acc = bank()
            product(acc[:, :width], w1_codes, w1_plane, t, xg_codes[:, cols], xg_plane[:, cols])
            nc.scalar.activation(out=y_win[t][:, cols], in_=acc[:, :width], func=ACT.Copy, scale=gain[:, t : t + 1])

        h_rows = kept([P, PACK, S], F32, "h_rows")
        h_win = [kept([P, S], F32, "h_win%d" % t) for t in range(PACK)]
        z_codes = kept([P, S], U32, "z_codes")
        z_plane = kept([P, S], U8, "z_plane")
        z_woven = [kept([P, HALF, PACK], BF16, "z_woven%d" % g) for g in range(2)]

        def spread(g, u, a_tag=None, d1_tag=None, d2_tag=None):
            name = "%d_%d" % (g, u)
            a = kept([P, 2, HALF], F32, "a" + name, a_tag)
            d1 = kept([P, 2, HALF], F32, "d1_" + name, d1_tag)
            d2 = kept([P, 2, HALF], F32, "d2_" + name, d2_tag)
            hi, lo = [kept([P, 2, HALF], F32, s + name) for s in ("hi", "lo")]
            for e in range(2):
                nc.vector.tensor_copy(out=a[:, e, :], in_=y_win[2 * u + e][:].indirect(entries(n1_t, HALF * g, HALF)))
            for d, lst in ((d1, n2_t), (d2, n3_t)):
                for e in range(2):
                    nc.vector.tensor_tensor(
                        out=d[:, e, :], in0=y_win[2 * u + e][:].indirect(entries(lst, HALF * g, HALF)), in1=a[:, e, :], op=ALU.subtract
                    )
            for ext, op in ((hi, ALU.max), (lo, ALU.min)):
                nc.vector.scalar_tensor_tensor(out=ext[:], in0=d1[:], scalar=0.0, in1=d2[:], op0=op, op1=op)
            return a, hi, lo

        def sum_on_tensor(g, u, a, hi, lo):
            name = "%d_%d" % (g, u)
            scaled = kept([P, 2, 2, HALF], F32, "scaled" + name)
            hi_c, lo_c = scaled[:, 0, :, :], scaled[:, 1, :, :]
            total = psum_t.tile([P, 2, 2, P], F32, name="total")
            for e in range(2):
                t = 2 * u + e
                for ext_c, ext, coef in ((hi_c, hi, c_max), (lo_c, lo, c_min)):
                    nc.scalar.activation(out=ext_c[:, e, :], in_=ext[:, e, :], func=ACT.Copy, scale=coef[:, t : t + 1])
                for blk in range(2):
                    for i, term in enumerate((a, hi_c, lo_c)):
                        nc.tensor.matmul(
                            total[:, blk, e, :], lhsT=term[:, e, P * blk : P * (blk + 1)], rhs=ident[:],
                            is_transpose=True, start=(i == 0), stop=(i == 2),
                        )
            return total

        def turn_back(g, u, total, back):
            z_t = kept([P, 2, P, 2], BF16, "z_t%d_%d" % (g, u))
            nc.scalar.activation(out=z_t[:], in_=total[:].rearrange("j b e p -> j b p e"), func=ACT.Copy, scale=0.5)
            z_t_words = z_t[:].rearrange("j b p e -> j (b p e)").bitcast(F32)
            for blk in range(2):
                nc.tensor.transpose(back[:, u, P * blk : P * (blk + 1)], z_t_words[:, P * blk : P * (blk + 1)], ident[:])

        def sum_on_vector(u, twice_z, pieces, a, hi, lo):
            part = kept([P, 2, HALF], F32, "part%d" % u)
            for e in range(2):
                t = 2 * u + e
                nc.vector.scalar_tensor_tensor(
                    out=part[:, e, :], in0=hi[:, e, :], scalar=c_max[:, t : t + 1], in1=a[:, e, :], op0=ALU.mult, op1=ALU.add
                )
            for js in pieces:
                for e in range(2):
                    t = 2 * u + e
                    nc.vector.scalar_tensor_tensor(
                        out=twice_z[:, t, js], in0=lo[:, e, js], scalar=c_min[:, t : t + 1], in1=part[:, e, js], op0=ALU.mult, op1=ALU.add
                    )

        def second_product(g, start, width):
            cols = slice(HALF * g + start, HALF * g + start + width)
            nc.vector.quantize_mx(
                out=z_codes[:, cols].bitcast(FP8X4), scales=z_plane[:, cols],
                in_=z_woven[g][:, start : start + width, :].rearrange("p j t -> p (j t)"),
            )
            accs = []
            for u in range(2):
                acc = bank()[:][:, : 2 * width].rearrange("p (e j) -> p e j", e=2)
                for e in range(2):
                    product(acc[:, e, :], w2_codes, w2_plane, 2 * u + e, z_codes[:, cols], z_plane[:, cols])
                accs.append(acc)
            return cols, accs

        def windows_on_scalar(u, cols, acc):
            pos = kept([P, 2, cols.stop - cols.start], F32, "pos%d_%d" % (cols.start, u))
            nc.scalar.activation(out=pos[:], in_=acc, func=ACT.Relu, scale=0.5)
            for e in range(2):
                nc.scalar.activation(out=h_win[2 * u + e][:, cols], in_=pos[:, e, :], func=ACT.Copy, scale=-1.0)

        def windows_on_vector(u, cols, acc):
            for e in range(2):
                nc.vector.tensor_scalar(
                    out=h_win[2 * u + e][:, cols], in0=acc[:, e, :], scalar1=0.0, scalar2=-0.5, op0=ALU.max, op1=ALU.mult
                )

        def keep_h(cols, accs):
            for u in range(2):
                nc.scalar.copy(out=h_rows[:, 2 * u : 2 * u + 2, cols], in_=accs[u])

        back = psum_t.tile([P, 2, HALF], F32, name="back")
        for u in range(2):
            turn_back(0, u, sum_on_tensor(0, u, *spread(0, u)), back)
        woven_words = z_woven[0][:].rearrange("p j t -> p (j t)").bitcast(F32).rearrange("p (j u) -> p j u", u=2)
        nc.scalar.copy(out=woven_words, in_=back[:].rearrange("p u j -> p j u"))

        twice_z = kept([P, PACK, HALF], F32, "z")
        blocks = [slice(P * blk, P * (blk + 1)) for blk in range(2)]
        sum_on_vector(0, twice_z, [slice(0, HALF)], *spread(1, 0, a_tag="d1_0_0", d1_tag="d1_0_1", d2_tag="d2_0_1"))
        cols, accs = second_product(0, 0, HALF)
        for u in range(2):
            windows_on_scalar(u, cols, accs[u])
        keep_h(cols, accs)
        sum_on_vector(1, twice_z, blocks, *spread(1, 1, d1_tag="z_woven0"))
        for js in blocks:
            nc.vector.tensor_scalar(
                out=z_woven[1][:, js, :].rearrange("p (c i) t -> p c t i", i=RUN),
                in0=twice_z[:, :, js].rearrange("p t (c i) -> p c t i", i=RUN),
                scalar1=0.5, scalar2=None, op0=ALU.mult,
            )
        late = [second_product(1, js.start, P) for js in blocks]
        for cols, accs in late:
            windows_on_vector(0, cols, accs[0])
            windows_on_scalar(1, cols, accs[1])
        for cols, accs in late:
            keep_h(cols, accs)

        out_rows = out_0.rearrange("(p t) s -> p t s", t=PACK)
        out_words = out_1[0].rearrange("p n t -> p (n t)").bitcast(I32)
        o_codes = kept([P, S], I32, "o_codes")
        o_plane = kept([P, S], U8, "o_plane")
        for n, (start, width) in enumerate(OUT_CHUNKS):
            cols = slice(start, start + width)
            o = kept([P, PACK, width], F32, "o%d" % n)
            for t in range(PACK):
                nc.vector.tensor_tensor(
                    out=o[:, t, :], in0=h_win[t][:].indirect(entries(n4_t, start, width)), in1=h_rows[:, t, cols], op=ALU.add
                )
            nc.sync.dma_start(out=out_rows[:, :, cols], in_=o[:])
            o_woven = kept([P, width * PACK], BF16, "o_woven%d" % n)
            nc.scalar.copy(
                out=o_woven[:].rearrange("p (c i t) -> p c t i", i=RUN, t=PACK), in_=o[:].rearrange("p t (c i) -> p c t i", i=RUN)
            )
            nc.vector.quantize_mx(out=o_codes[:, cols].bitcast(FP8X4), scales=o_plane[:, cols], in_=o_woven[:])
            nc.sync.dma_start(out=out_words[:, cols], in_=o_codes[:, cols])
        for q in range(QUADRANTS):
            queue = nc.sync if q % 2 == 0 else nc.scalar
            queue.dma_start(out=out_2[0, 4 * q : 4 * q + 4, :].bitcast(I32), in_=o_plane[32 * q : 32 * q + 4, :].bitcast(I32))
